import numpy as np, ml_dtypes
CORES = [23,119,17,113]
N = 4
import mx_ref
BF = ml_dtypes.bfloat16
def gentries(a):
    return np.ascontiguousarray(a.reshape(8, 16, -1).transpose(0, 2, 1)).reshape(8, -1)
def gtable(e):
    e = np.asarray(e); return np.ascontiguousarray(e.reshape(8, -1, 16).transpose(0, 2, 1)).reshape(128, -1).astype(np.int32)
def gcols(t, e):
    v = np.concatenate([t.reshape(8, 16, -1, 4), np.zeros((8, 16, 1, 4), BF)], axis=2)
    return np.ascontiguousarray(np.stack([v[g][:, e[g]] for g in range(8)])).reshape(128, -1)
def gpick(z, e):
    return np.concatenate([z[16 * g:16 * g + 16][:, e[g]] for g in range(8)])
def f(rng, *shape):
    return mx_ref.flush((rng.standard_normal(shape, dtype=np.float32) * np.exp2(rng.integers(-2, 3, shape[:-1] + (1,)))).astype(BF))
def wide(rng, *shape, cols=0):
    v = rng.standard_normal(shape, dtype=np.float32) * np.exp2(rng.integers(-12, 13, shape)).astype(np.float32)
    if cols: v *= np.repeat(np.exp2(rng.integers(-cols, cols + 1, shape[:-2] + (1, shape[-1] // 4))) * (rng.random(shape[:-2] + (1, shape[-1] // 4)) > 0.0625), 4, axis=-1).astype(np.float32)
    return mx_ref.flush(v.astype(BF))
T, CAPP, NB, KK = 1024, 192, 4, 256
MASK = np.repeat(np.arange(128)[:, None] // 16 == np.arange(128)[None] // 16, 4, axis=1)
def lists(rng, agree=False, one=False, full=False, repeat=False):
    a, o = [], []
    for r in range(N):
        n = rng.integers(0, CAPP + 1, (8, N))
        far, most, none = -1, -1, -1
        if one:
            far = (r + rng.integers(1, N)) % N; most, none = rng.permutation(8)[:2]
            n[most, far] = CAPP; n[none, far] = 0
        if full: n[:] = CAPP
        n[n.sum(axis=1) == 0, r] = 1
        e = np.full((8, N, CAPP), -1)
        for g in range(8):
            for q in range(N):
                v = rng.integers(0, T, n[g, q])
                if one and g == most and q == far: v = rng.permutation(T)[:CAPP]
                if full: v[0] = 0; v[1] = T - 1
                e[g, q, rng.permutation(CAPP)[:n[g, q]]] = v
        if agree: e = np.stack([e[0]] * 8)
        e = e.reshape(8, -1); used = [np.flatnonzero(e[g] >= 0) for g in range(8)]
        k = np.stack([np.full(KK, rng.choice(u)) if repeat else rng.choice(u, KK) for u in used])
        if one: k[most, rng.permutation(KK)[:CAPP]] = far * CAPP + rng.permutation(CAPP)
        if full: k[:, 0] = 0; k[:, -1] = N * CAPP - 1
        a.append(gtable(e)); o.append(gtable(k))
    return {"rq": np.stack(a), "od": np.stack(o)}
def setup_inputs(rng):
    ky = f(rng, N, 128, 4 * T); qd = np.array(f(rng, N, 128, NB * 512))
    qd[:, ~np.concatenate([MASK] * NB, axis=1)] = 0
    return {"ky": ky, "qd": qd, **lists(rng)}
def setup_inputs_agree(rng):
    return {**setup_inputs(rng), **lists(rng, agree=True)}
def setup_inputs_one(rng):
    return {**setup_inputs(rng), **lists(rng, one=True)}
def setup_inputs_full(rng):
    return {**setup_inputs(rng), **lists(rng, full=True)}
def setup_inputs_repeat(rng):
    return {**setup_inputs(rng), **lists(rng, repeat=True)}
def setup_inputs_spread(rng):
    d = setup_inputs(rng); d["ky"] = wide(rng, N, 128, 4 * T, cols=8); return d
def check_inputs(d):
    b = []
    for r in range(N):
        e, o = gentries(d["rq"][r]), gentries(d["od"][r])
        if e.min() < -1 or e.max() >= T: b.append("rq")
        if o.min() < 0 or o.max() >= N * CAPP or (np.take_along_axis(e, np.clip(o, 0, N * CAPP - 1), axis=1) < 0).any(): b.append("od")
        if not (d["qd"][r][~np.concatenate([MASK] * NB, axis=1)].astype(np.float32) == 0).all(): b.append("qd")
    return b
def reference(ky, qd, rq, od):
    y = np.zeros((N, 128, NB * KK), np.float32)
    for r in range(N):
        e, o = gentries(rq[r]), gentries(od[r])
        slots = mx_ref.quantize(np.concatenate([gcols(ky[q], e[:, q * CAPP:(q + 1) * CAPP]) for q in range(N)], axis=1))
        for b in range(NB):
            z = mx_ref.matmul(mx_ref.quantize(np.ascontiguousarray(qd[r][:, 512 * b:512 * b + 512])), slots)
            y[r][:, KK * b:KK * b + KK] = gpick(z, o)
    return {"y": y}

from concourse.bass import DstId, RemoteDMATransfer
from concourse.mybir import dt, AluOpType, ActivationFunctionType

NR, T_KEYS, CAPP, NB, KK = 4, 1024, 192, 4, 256
LC = CAPP // 16
PAD = 16
ROLES = ["O", "A", "C", "B"]
POS = {"O": 0, "A": 1, "C": 2, "B": 3}
SRC = {"A": 0, "B": 1, "C": 2}

SCRATCH = {
    "rqs": ("sbuf", [128, NR, LC], "int32"),
    "own": ("sbuf", [128, NR, 2 * LC], "uint16"),
    "kyb": ("sbuf", [128, PAD + 4 * T_KEYS], "bfloat16"),
    "qdb": ("sbuf", [128, NB * 512], "bfloat16"),
    "ods": ("sbuf", [128, KK // 16], "int32"),
    "odu": ("sbuf", [128, KK // 16], "uint16"),
    "cout": ("sbuf", [128, 3 * CAPP], "float8_e4m3fn_x4"),
    "pout": ("sbuf", [128, 3 * CAPP], "uint8"),
    "scod": ("sbuf", [128, NR * CAPP], "float8_e4m3fn_x4"),
    "spla": ("sbuf", [128, NR * CAPP], "uint8"),
    "qcod": ("sbuf", [128, NB * 128], "float8_e4m3fn_x4"),
    "qpla": ("sbuf", [128, NB * 128], "uint8"),
    "yout": ("sbuf", [128, NB * KK], "float32"),
    "ps": ("psum", [128, 512 * 8], "float32"),
}
for _x in "OABC":
    SCRATCH["h" + _x] = ("sbuf", [128, 4 * CAPP], "bfloat16")
    SCRATCH["one" + _x] = ("sbuf", [128, 2 * LC], "uint16")
for _x in "ABC":
    SCRATCH["lst" + _x] = ("sbuf", [128, 2 * LC], "uint16")
for _b in range(NB):
    SCRATCH["z%d" % _b] = ("sbuf", [128, NR * CAPP], "float32")

SEMAPHORES = (["ldrq", "ldky", "ldqd", "ldod", "pad", "mine", "lsent", "csent", "qdq", "odc", "stored"]
              + ["list" + x for x in "ABC"] + ["arr" + x for x in "ABC"]
              + ["plus" + x for x in "OABC"] + ["gath" + x for x in "OABC"] + ["quan" + x for x in "OABC"]
              + ["mm%s%d" % (x, b) for x in "OABC" for b in range(NB)]
              + ["cp%s%d" % (x, b) for x in "OABC" for b in range(NB)]
              + ["pick%d" % b for b in range(NB)])


def rank_program(g, core, T, topo):
    rank = T.rank_of(core)
    if rank is None:
        return
    V, S, X = g.vector, g.scalar, g.sync
    sem = T.sem

    role = {"O": rank}
    for q, c in enumerate(T.cores):
        if q == rank:
            continue
        if topo.chip(c) == topo.chip(core):
            role["C"] = q
        elif topo.die(c) == topo.die(core):
            role["A"] = q
        else:
            role["B"] = q
    off = [e for e in topo.engines(core, T.cores[role["A"]]) if e in topo.engines(core, T.cores[role["B"]])]
    on = [e for e in topo.engines(core, T.cores[role["C"]]) if e not in off]
    half = len(off) // 2

    def addr(x):
        rid, pid, _ = topo.addr(T.cores[role[x]])
        return rid, pid

    def mask(engines):
        m = 0
        for e in engines:
            m |= 1 << e
        return m

    list_eng = {"A": off[:half], "B": off[half:], "C": on}
    code_eng = {"A": off, "B": off, "C": on}

    def lists(x):
        if x == "O":
            return lambda i: T.own[:, rank, i * LC:(i + 1) * LC]
        return lambda i: T["lst" + x][:, i * LC:(i + 1) * LC]

    def wait_list(eng, x):
        if x == "O":
            eng.wait_ge(sem.mine, 2)
        else:
            eng.wait_ge(sem["list" + x], len(list_eng[x]))

    X.dma_start(T.rqs[:], T.rq[:]).then_inc(sem.ldrq, 16)
    X.dma_start(T.kyb[:, PAD:PAD + 4 * T_KEYS], T.ky[:]).then_inc(sem.ldky, 16)
    X.wait_ge(sem.ldky, 16)
    X.dma_start(T.qdb[:], T.qd[:]).then_inc(sem.ldqd, 16)
    X.dma_start(T.ods[:], T.od[:]).then_inc(sem.ldod, 16)

    V.memset(T.kyb[:, 0:PAD], 0.0).then_inc(sem["pad"], 1)
    V.wait_ge(sem.ldrq, 16)
    for i in range(2):
        V.tensor_scalar(T.own[:, :, i * LC:(i + 1) * LC], T.rqs[:], 4, PAD + 2 * i,
                        AluOpType.mult, AluOpType.add).then_inc(sem.mine, 1)

    g.wait_ge(sem.mine, 2)
    tr = []
    for x in "ABC":
        rid, pid = addr(x)
        tr.append(RemoteDMATransfer(dst_ids=[DstId(rid=rid, pnc=pid)], dma_engine_mask=mask(list_eng[x]),
                                    remote_sem=sem["list" + x], src=T.own[:, role[x], :], dst=T["lst" + x][:]))
    g.remote_dma_fused(tr, local_sem=sem.lsent)

    win = T.kyb[:, 0:PAD + 4 * T_KEYS]
    S.wait_ge(sem["pad"], 1)
    S.wait_ge(sem.ldky, 16)
    V.wait_ge(sem["pad"], 1)
    V.wait_ge(sem.ldky, 16)

    def gather(eng, x, t):
        offs = lists(x)(t // 2) if t % 2 == 0 else T["one" + x][:, (t // 2) * LC:(t // 2 + 1) * LC]
        out = T["h" + x][:, t:4 * CAPP:4]
        if eng == "V":
            V.tensor_copy(out, win.indirect(offs)).then_inc(sem["gath" + x], 1)
        else:
            S.activation(out, win.indirect(offs), ActivationFunctionType.Copy).then_inc(sem["gath" + x], 1)

    def keys(x, vec, sca):
        wait_list(V, x)
        src = T.own[:, rank, :] if x == "O" else T["lst" + x][:]
        V.tensor_scalar(T["one" + x][:], src, 1, None, AluOpType.add).then_inc(sem["plus" + x], 1)
        seen = False
        for t in vec:
            if t % 2 and not seen:
                V.wait_ge(sem["plus" + x], 1)
                seen = True
            gather("V", x, t)
        wait_list(S, x)
        seen = False
        for t in sca:
            if t % 2 and not seen:
                S.wait_ge(sem["plus" + x], 1)
                seen = True
            gather("S", x, t)
        V.wait_ge(sem["gath" + x], 4)
        if x == "O":
            a = POS[x] * CAPP
            V.quantize_mx(T.scod[:, a:a + CAPP], T.spla[:, a:a + CAPP], T["h" + x][:]).then_inc(sem["quan" + x], 1)
        else:
            a = SRC[x] * CAPP
            V.quantize_mx(T.cout[:, a:a + CAPP], T.pout[:, a:a + CAPP], T["h" + x][:]).then_inc(sem["quan" + x], 1)

    for x in "ABC":
        keys(x, [0, 1], [2, 3])
        rid, pid = addr(x)
        a, d, m = SRC[x] * CAPP, POS[x] * CAPP, mask(code_eng[x])
        g.wait_ge(sem["quan" + x], 1)
        g.remote_dma(T.scod[:, d:d + CAPP].bitcast(dt.uint8), T.cout[:, a:a + CAPP].bitcast(dt.uint8),
                     sem["arr" + x], sem.csent, pid, rid, m)
        g.remote_dma(T.spla[:, d:d + CAPP], T.pout[:, a:a + CAPP],
                     sem["arr" + x], sem.csent, pid, rid, m)

    V.wait_ge(sem.ldqd, 16)
    V.quantize_mx(T.qcod[:], T.qpla[:], T.qdb[:]).then_inc(sem.qdq, 1)
    keys("O", [0], [2, 1, 3])
    V.wait_ge(sem.ldod, 16)
    V.tensor_copy(T.odu[:], T.ods[:]).then_inc(sem.odc, 1)

    g.tensor.wait_ge(sem.qdq, 1)
    for k, x in enumerate(ROLES):
        if x == "O":
            g.tensor.wait_ge(sem.quanO, 1)
        else:
            g.tensor.wait_ge(sem["arr" + x], 2 * len(code_eng[x]))
        a = POS[x] * CAPP
        for b in range(NB):
            bank = 512 * (NB * (k % 2) + b)
            if k >= 2:
                g.tensor.wait_ge(sem["cp%s%d" % (ROLES[k - 2], b)], 1)
            g.tensor.matmul_mx(T.ps[:, bank:bank + CAPP], T.qcod[:, 128 * b:128 * b + 128],
                               T.qpla[:, 128 * b:128 * b + 128], T.scod[:, a:a + CAPP], T.spla[:, a:a + CAPP],
                               True, True).then_inc(sem["mm%s%d" % (x, b)], 1)

    def copy(x, k, b):
        bank = 512 * (NB * (k % 2) + b)
        eng = S if b % 2 else V
        eng.wait_ge(sem["mm%s%d" % (x, b)], 1)
        out, in_ = T["z%d" % b][:, role[x] * CAPP:(role[x] + 1) * CAPP], T.ps[:, bank:bank + CAPP]
        if b % 2:
            S.activation(out, in_, ActivationFunctionType.Copy).then_inc(sem["cp%s%d" % (x, b)], 1)
        else:
            V.tensor_copy(out, in_).then_inc(sem["cp%s%d" % (x, b)], 1)

    for k, x in enumerate(ROLES[:-1]):
        for b in range(NB):
            copy(x, k, b)
    V.wait_ge(sem.odc, 1)
    S.wait_ge(sem.odc, 1)
    for b in range(NB):
        copy(ROLES[-1], NB - 1, b)
        eng = S if b % 2 else V
        for x in ROLES:
            eng.wait_ge(sem["cp%s%d" % (x, b)], 1)
        pick = T["z%d" % b][:, 0:NR * CAPP].indirect(T.odu[:, 0:KK // 16])
        out = T.yout[:, b * KK:(b + 1) * KK]
        if b % 2:
            S.activation(out, pick, ActivationFunctionType.Copy).then_inc(sem["pick%d" % b], 1)
        else:
            V.tensor_copy(out, pick).then_inc(sem["pick%d" % b], 1)
        X.wait_ge(sem["pick%d" % b], 1)
        X.dma_start(T.y[:, b * KK:(b + 1) * KK], T.yout[:, b * KK:(b + 1) * KK]).then_inc(sem.stored, 16)

    g.wait_ge(sem.lsent, sum(len(list_eng[x]) for x in "ABC"))
    g.wait_ge(sem.csent, sum(2 * len(code_eng[x]) for x in "ABC"))
    X.wait_ge(sem.stored, 16 * NB)
